import numpy as np
import ml_dtypes


def mxq(x, axis, fmt="e4m3"):
    dtype, down = {"e4m3": (ml_dtypes.float8_e4m3fn, 7), "e5m2": (ml_dtypes.float8_e5m2, 14)}[fmt]
    v = np.moveaxis(np.asarray(x, np.float32).astype(ml_dtypes.bfloat16).astype(np.float64), axis, -1)
    blocks = v.reshape(v.shape[:-1] + (-1, 32))
    amax = np.abs(blocks).max(-1, keepdims=True)
    byte = np.maximum(np.where(amax > 0, np.frexp(amax)[1] - 1 + 127, 0) - down, 1)
    scale = np.exp2(byte - 127.0)
    codes = (blocks / scale).astype(np.float32).astype(dtype).astype(np.float64)
    return np.moveaxis((codes * scale).reshape(v.shape), -1, axis)


WIDE = False


def mx_kscale(k):
    if not WIDE:
        return np.ones(k)
    levels = np.array([10, -10, 5, -5, 0])
    if k % 512:
        return np.exp2(np.random.permutation(np.resize(levels, k // 32))).repeat(32)
    a = np.empty((k // 512, 16))
    for p in range(k // 512):
        a[p, :8] = np.random.permutation(np.resize(levels, 8))
        for g in range(8):
            far = levels[np.abs(levels - a[p, g]) >= 10]
            a[p, g + 8] = far[np.random.randint(len(far))]
    return np.exp2(a.ravel()).repeat(32)


BF16 = ml_dtypes.bfloat16


def bf(x):
    return np.asarray(x, np.float32).astype(BF16)


def f64(x):
    return np.asarray(x).astype(np.float64)


E2M1 = np.array([0.0, 0.5, 1.0, 1.5, 2.0, 3.0, 4.0, 6.0, -0.0, -0.5, -1.0, -1.5, -2.0, -3.0, -4.0, -6.0])


def pack_weight(w, fmt):
    k, n = w.shape
    w = f64(bf(w)).reshape(k // 32, 32, n)
    amax = np.abs(w).max(1)
    if fmt == "e4m3":
        byte = np.frexp(amax)[1] - 1 + 127 - 7
    else:
        mant, ex = np.frexp(amax / 6.0)
        byte = np.where(mant > 0.5, ex, ex - 1) + 127
    byte = np.clip(np.where(amax > 0, byte, 1), 1, 254)
    scaled = (w * np.exp2(127.0 - byte)[:, None, :]).reshape(k, n).astype(np.float32)
    by_word = np.ascontiguousarray(scaled.reshape(k // 512, 128, 4, n).transpose(0, 1, 3, 2))
    if fmt == "e4m3":
        words = by_word.astype(ml_dtypes.float8_e4m3fn).view(np.uint8)
    else:
        c = by_word.astype(ml_dtypes.float4_e2m1fn).view(np.uint8) & 0xF
        words = c[..., 0::2] | (c[..., 1::2] << 4)
    return np.ascontiguousarray(words), np.ascontiguousarray(byte.astype(np.uint8).reshape(k // 512, 16, n))


def unpack_weight(words, scales, fmt):
    g, p, n, _ = words.shape
    if fmt == "e4m3":
        vals = np.ascontiguousarray(words).view(ml_dtypes.float8_e4m3fn).astype(np.float64)
    else:
        nib = np.empty((g, p, n, 4), np.uint8)
        nib[..., 0::2] = words & 0xF
        nib[..., 1::2] = words >> 4
        vals = E2M1[nib]
    vals = vals * np.repeat(np.exp2(scales.astype(np.float64) - 127.0), 8, axis=1)[..., None]
    return vals.transpose(0, 1, 3, 2).reshape(g * 512, n)
def pack4(w):
    words, scales = pack_weight(w, "e2m1")
    return words.reshape(words.shape[0], 128, -1), scales


def unpack4(words, scales):
    return unpack_weight(words.reshape(words.shape[0], 128, -1, 2), scales, "e2m1")


def planes(Y):
    n, m = Y.shape
    b = f64(bf(Y)).reshape(n // 32, 32, m)
    amax = np.abs(b).max(1)
    byte = np.clip(np.where(amax > 0, np.frexp(amax)[1] - 1 + 127 - 7, 1), 1, 254)
    codes = (b * np.exp2(127.0 - byte)[:, None, :]).reshape(n, m).astype(np.float32).astype(ml_dtypes.float8_e4m3fn).view(np.uint8)
    words = codes.reshape(n // 512, 128, 4, m).transpose(0, 1, 3, 2)
    return np.ascontiguousarray(words), np.ascontiguousarray(byte.astype(np.uint8).reshape(n // 512, 16, m))


N1, N2, J, K, C, Q = 512, 1024, 1024, 1536, 512, 32
NS = N1 + N2
BIAS = NS / (NS - 1.0)

def standard(x):
    return (x - x.mean(axis=0)) / x.std(axis=0)

def cohort(rows):
    hap = 0.3 * np.random.randn(rows, Q)
    x = np.repeat(hap, J // Q, axis=1) + np.random.randn(rows, J)
    p = np.repeat(hap, K // Q, axis=1) + np.random.randn(rows, K)
    return standard(x), standard(p) / np.sqrt(NS)

def setup_inputs():
    s1, s2, t = mx_kscale(N1), mx_kscale(N2), mx_kscale(K)
    x1, p1 = cohort(N1)
    x2, p2 = cohort(N2)
    p2_words, p2_scales = pack4(p2 / s2[:, None])
    w = np.exp(0.3 * np.random.randn(K)) * (NS - 1.0) / (NS - 2.0)
    annot = np.random.randn(K, C) / np.sqrt(K)
    return {"x1": bf(x1 * s1[:, None]), "p1": bf(p1 / s1[:, None]),
            "x2": bf(x2 * s2[:, None]), "p2_words": p2_words, "p2_scales": p2_scales,
            "w": bf(w * t), "annot": bf(annot / t[:, None]),
            "l0": bf(np.random.randn(J, C)), "v": bf(np.exp(0.8 * np.random.randn(J)))}

def reference(x1, p1, x2, p2_words, p2_scales, w, annot, l0, v):
    Z = ((mxq(f64(x1), 0, "e4m3").T @ mxq(f64(p1), 0, "e4m3"))
         + (mxq(f64(x2), 0, "e4m3").T @ unpack4(p2_words, p2_scales)))
    H = (Z * Z - BIAS) * f64(w)
    L = mxq(H, 1, "e4m3") @ mxq(f64(annot), 0, "e4m3")
    y = (L + f64(l0)) * f64(v)[:, None]
    Y = y
    words, scales = planes(Y)
    return y, words, scales

from contextlib import ExitStack

import concourse.mybir as mybir
from concourse.masks import make_identity

N1, N2, J, K, C = 512, 1024, 1024, 1536, 512
BIAS = (N1 + N2) / (N1 + N2 - 1.0)
FLOPS = 2 * J * K * (N1 + N2) + 2 * J * K * C

F32 = mybir.dt.float32
BF16 = mybir.dt.bfloat16
I32 = mybir.dt.int32
U32 = mybir.dt.uint32
U8 = mybir.dt.uint8
FP8X4 = mybir.dt.float8_e4m3fn_x4
FP4X4 = mybir.dt.float4_e2m1fn_x4
ALU = mybir.AluOpType
ACT = mybir.ActivationFunctionType

P = 128
W = 512
G = K // W
H = J // W


def tile_annotated_ld_scores_k6_kernel(tc, x1, p1, x2, p2_words, p2_scales, w, annot, l0, v, out_0, out_1, out_2):
    nc = tc.nc
    with ExitStack() as ctx:
        keep = ctx.enter_context(tc.tile_pool(name="keep", bufs=1))
        stage = ctx.enter_context(tc.tile_pool(name="stage", bufs=4))
        zpool = ctx.enter_context(tc.psum_pool(name="zpool", bufs=4))
        lpool = ctx.enter_context(tc.psum_pool(name="lpool", bufs=4))
        ctx.enter_context(tc.manual_schedule())

        def kept(name, shape, dtype):
            return keep.tile(shape, dtype, name=name, align_bytes=64)

        raw, codes, scales, grouped = {}, {}, {}, {}
        x_rows = [x2[0:W, :], x2[W : 2 * W, :], x1]
        engines = {"V": nc.vector, "S": nc.scalar, "G": nc.gpsimd}

        def move(e, out, in_):
            if e == "V":
                nc.vector.tensor_copy(out=out, in_=in_)
            elif e == "S":
                nc.scalar.copy(out=out, in_=in_)
            else:
                nc.gpsimd.tensor_scalar(out=out, in0=in_, scalar1=1.0, scalar2=0.0, op0=ALU.mult, op1=ALU.add)

        def load_rows(key, rows):
            raw[key] = kept("raw_%s%d%d" % key, [P, 4, W], BF16)
            nc.sync.dma_start(out=raw[key][:], in_=rows.rearrange("(p j) c -> p j c", j=4))

        def load_x(a, h):
            load_rows(("x", a, h), x_rows[a][:, h * W : (h + 1) * W])

        def load_p1(g):
            load_rows(("p", g, 0), p1[:, g * W : (g + 1) * W])

        def load_l0(h):
            load_rows(("l", h, 0), l0[h * W : (h + 1) * W, :])

        def load_a(g):
            key = ("a", g, 0)
            raw[key] = kept("raw_%s%d%d" % key, [P, 4, W], BF16)
            rows = annot[g * W : (g + 1) * W, :].rearrange("(u t i) c -> i u t c", t=4, i=4)
            for i in range(4):
                nc.sync.dma_start(out=raw[key][i:P:4, :, :], in_=rows[i])

        p2_raw, p2_codes, p2_planes = {}, {}, {}
        s2_first = kept("s2_first", [P, 2, W], U8)
        s2_rest = kept("s2_rest", [P, 2, K - W], U8)

        def load_p2(g):
            p2_raw[g] = kept("p2_raw%d" % g, [P, 2, 2 * W], U8)
            src = p2_words[:, :, 2 * W * g : 2 * W * (g + 1)].bitcast(I32).rearrange("a p n -> p a n")
            nc.sync.dma_start(out=p2_raw[g][:].bitcast(I32), in_=src)

        def load_p2_scales(dst, n0, n1):
            for q in range(4):
                src = p2_scales[:, 4 * q : 4 * q + 4, n0:n1].bitcast(I32).rearrange("a r n -> r a n")
                nc.sync.dma_start(out=dst[32 * q : 32 * q + 4, :, :].bitcast(I32), in_=src)

        def order_p2(g):
            p2_codes[g] = kept("p2_codes%d" % g, [P, 2, 2 * W], U8)
            p2_planes[g] = kept("p2_planes%d" % g, [P, 2, W], U8)
            src = s2_first[:] if g == 0 else s2_rest[:, :, (g - 1) * W : g * W]
            nc.vector.tensor_copy(
                out=p2_planes[g][:].bitcast(I32).rearrange("p a (t u) -> p a t u", t=4),
                in_=src.bitcast(I32).rearrange("p a (u t) -> p a t u", t=4),
            )
            nc.vector.tensor_copy(
                out=p2_codes[g][:].bitcast(I32).rearrange("p a (t u e) -> p a t u e", t=4, e=2),
                in_=p2_raw[g][:].bitcast(I32).rearrange("p a (u t e) -> p a t u e", t=4, e=2),
            )

        def group_tile(key):
            if key not in grouped:
                grouped[key] = stage.tile([P, W, 4], BF16, name="grouped", align_bytes=64, bufs=9)
                codes[key] = kept("codes_%s%d%d" % key, [P, W], U32)
                scales[key] = kept("scales_%s%d%d" % key, [P, W], U8)
            return grouped[key]

        def interleave(key, e, c0, c1, src=None):
            src = raw[key] if src is None else src
            dst = group_tile(key)
            if key[0] == "p":
                for t in range(c0 // P, c1 // P):
                    move(
                        e,
                        dst[:, t * P : (t + 1) * P, :].rearrange("p (u i) j -> p u j i", i=4),
                        src[:].rearrange("p j (u t i) -> p t u j i", t=4, i=4)[:, t],
                    )
            else:
                move(
                    e,
                    dst[:, c0:c1, :].rearrange("p (c i) j -> p c j i", i=4),
                    src[:, :, c0:c1].rearrange("p j (c i) -> p c j i", i=4),
                )

        def quantize(key, c0=0, c1=W):
            nc.vector.quantize_mx(
                out=codes[key][:, c0:c1].bitcast(FP8X4),
                scales=scales[key][:, c0:c1],
                in_=grouped[key][:, c0:c1, :].rearrange("p c j -> p (c j)"),
            )

        z_banks, squares, weighted = {}, {}, {}

        def z_pass(g, h, t, a):
            if a == 0:
                z_banks[g, h, t] = zpool.tile([P, W], F32, name="z_bank")
            cols = slice(t * P, (t + 1) * P)
            if a < 2:
                lhs = p2_codes[g][:, a, 2 * t * P : 2 * (t + 1) * P].bitcast(FP4X4)
                lhs_scale = p2_planes[g][:, a, cols]
            else:
                lhs = codes["p", g, 0][:, cols].bitcast(FP8X4)
                lhs_scale = scales["p", g, 0][:, cols]
            nc.tensor.matmul_mx(
                out=z_banks[g, h, t][:],
                lhsT=lhs,
                lhsT_scale=lhs_scale,
                rhs=codes["x", a, h][:].bitcast(FP8X4),
                rhs_scale=scales["x", a, h][:],
                start=(a == 0),
                stop=(a == 2),
            )

        def square(g, h, t):
            squares[g, h, t] = stage.tile([P, W], F32, name="square", align_bytes=64, bufs=8)
            nc.scalar.activation(
                out=squares[g, h, t][:].rearrange("p (s m) -> p s m", s=4),
                in_=z_banks[g, h, t][:].rearrange("p (m s) -> p s m", s=4),
                func=ACT.Square,
            )

        def weigh(g, h, t):
            if t == 0:
                raw["h", g, h] = stage.tile([P, 4, W], BF16, name="h_rows", align_bytes=64, bufs=3)
            nc.vector.tensor_scalar(
                out=raw["h", g, h][:, t, :],
                in0=squares[g, h, t][:],
                scalar1=BIAS,
                scalar2=w_cols[:, t, g : g + 1],
                op0=ALU.subtract,
                op1=ALU.mult,
            )

        l_banks, l0v = {}, {}

        def l_pass(h, s, g):
            if g == 0:
                l_banks[h, s] = lpool.tile([P, W], F32, name="l_bank")
            cols = slice(s * P, (s + 1) * P)
            nc.tensor.matmul_mx(
                out=l_banks[h, s][:],
                lhsT=codes["h", g, h][:, cols].bitcast(FP8X4),
                lhsT_scale=scales["h", g, h][:, cols],
                rhs=codes["a", g, 0][:].bitcast(FP8X4),
                rhs_scale=scales["a", g, 0][:],
                start=(g == 0),
                stop=(g == G - 1),
            )

        def scale_l0(h, s, e):
            l0v[h, s] = kept("l0v%d%d" % (h, s), [P, W], F32)
            if e == "S":
                nc.scalar.activation(out=l0v[h, s][:], in_=raw["l", h, 0][:, s, :], func=ACT.Copy, scale=v_cols[:, h, s : s + 1])
            else:
                engines[e].tensor_scalar(
                    out=l0v[h, s][:], in0=raw["l", h, 0][:, s, :], scalar1=v_cols[:, h, s : s + 1], scalar2=0.0, op0=ALU.mult, op1=ALU.add
                )

        def finish_y(h, s, c0=0, c1=W):
            if ("y", h, 0) not in raw:
                raw["y", h, 0] = kept("y%d" % h, [P, 4, W], F32)
            nc.vector.scalar_tensor_tensor(
                out=raw["y", h, 0][:, s, c0:c1],
                in0=l_banks[h, s][:, c0:c1],
                scalar=v_cols[:, h, s : s + 1],
                in1=l0v[h, s][:, c0:c1],
                op0=ALU.mult,
                op1=ALU.add,
            )

        def store_y(h, s):
            rows = out_0[h * W : (h + 1) * W, :].rearrange("(p s) c -> p s c", s=4)
            nc.sync.dma_start(out=rows[:, s, :], in_=raw["y", h, 0][:, s, :])

        def store_codes(h, c0=0, c1=W, q=None):
            dst = out_1[h].rearrange("p c s -> p (c s)").bitcast(I32)
            (q or nc.sync).dma_start(out=dst[:, c0:c1], in_=codes["y", h, 0][:, c0:c1].bitcast(I32))

        def store_scales(h, qs, q=None):
            for r in qs:
                (q or nc.sync).dma_start(
                    out=out_2[h, 4 * r : 4 * r + 4, :].bitcast(I32),
                    in_=scales["y", h, 0][32 * r : 32 * r + 4, :].bitcast(I32),
                )

        w_rows = kept("w_rows", [G, W], BF16)
        w_ordered = kept("w_ordered", [P, W], BF16)
        w_cols = kept("w_cols", [P, 4, 4], F32)
        v_raw = kept("v_raw", [P, H, 4], BF16)
        v_cols = kept("v_cols", [P, H, 4], F32)
        ident = kept("ident", [P, P], BF16)
        warm = kept("warm", [P, 2], F32)

        def setup():
            nc.vector.memset(s2_first[:].bitcast(I32), 0)
            nc.vector.memset(warm[:], 0.0)
            nc.vector.memset(s2_rest[:].bitcast(I32), 0)
            nc.vector.memset(w_ordered[:], 0.0)
            make_identity(nc, ident[:])
            nc.scalar.dma_start(out=w_rows[:], in_=w.rearrange("(g k) -> g k", g=G))
            nc.scalar.activation(out=warm[:, 1:2], in_=warm[:, 0:1], func=ACT.Square)

        def load_v():
            nc.sync.dma_start(out=v_raw[:], in_=v.rearrange("(h p s) -> p h s", h=H, s=4))

        def widen_v():
            nc.vector.tensor_copy(out=v_cols[:], in_=v_raw[:])

        def spread_w():
            nc.vector.tensor_copy(
                out=w_ordered[0:G, :].rearrange("g (t u i) -> g t u i", t=4, i=4),
                in_=w_rows[:].rearrange("g (u t i) -> g t u i", t=4, i=4),
            )
            w_bank = lpool.tile([P, 4, 4], F32, name="l_bank")
            for t in range(4):
                nc.tensor.matmul(out=w_bank[:, t, :], lhsT=w_ordered[:, t * P : (t + 1) * P], rhs=ident[:, 0:4], start=True, stop=True)
            nc.scalar.copy(out=w_cols[:], in_=w_bank[:])


        setup()
        load_x(0, 0)
        load_p2_scales(s2_first, 0, W)
        load_p2(0)
        load_x(1, 0)
        load_x(2, 0)
        load_p1(0)
        load_p2_scales(s2_rest, W, K)
        load_p2(1)
        load_p1(1)
        load_p2(2)
        load_p1(2)
        for a in range(3):
            load_x(a, 1)
        load_v()
        for g in range(G):
            load_a(g)
        for h in range(H):
            load_l0(h)
        spread_w()
        X = lambda a, h: ("x", a, h)
        PP = lambda g: ("p", g, 0)
        A = lambda g: ("a", g, 0)
        HH = lambda g, h: ("h", g, h)
        Y = lambda h: ("y", h, 0)
        il = interleave
        qz = quantize

        def z_tile(g, h, t):
            for a in range(3):
                z_pass(g, h, t, a)

        def phase(g, h, nxt, key, c0=0, c1=W):
            step = (c1 - c0) // 4
            for t in range(4):
                square(g, h, t)
                if nxt is not None:
                    z_tile(nxt[0], nxt[1], t)
                if key is not None:
                    il(key, "S", c0 + t * step, c0 + (t + 1) * step)

        def weigh_all(g, h):
            for t in range(4):
                weigh(g, h, t)
        il(('x', 0, 0), "V", 384, 512)
        il(('x', 0, 0), "V", 128, 256)
        il(('x', 0, 0), "V", 0, 128)
        il(('x', 0, 0), "V", 256, 384)
        qz(('x', 0, 0), 0, 256)
        qz(('x', 0, 0), 256, 512)
        order_p2(0)
        z_pass(0, 0, 0, 0)
        il(('x', 1, 0), "S", 256, 384)
        il(('x', 1, 0), "V", 128, 256)
        il(('x', 1, 0), "V", 0, 128)
        z_pass(0, 0, 1, 0)
        il(('x', 1, 0), "S", 384, 512)
        qz(('x', 1, 0), 0, 256)
        z_pass(0, 0, 2, 0)
        qz(('x', 1, 0), 256, 512)
        il(('x', 2, 0), "S", 384, 512)
        il(('x', 2, 0), "V", 256, 384)
        z_pass(0, 0, 1, 1)
        il(('x', 2, 0), "V", 0, 128)
        il(('x', 2, 0), "V", 128, 256)
        z_pass(0, 0, 2, 1)
        qz(('x', 2, 0), 256, 512)
        z_pass(0, 0, 0, 1)
        il(('p', 0, 0), "S", 0, 128)
        il(('p', 0, 0), "V", 256, 384)
        z_pass(0, 0, 3, 0)
        qz(('x', 2, 0), 0, 256)
        il(('p', 0, 0), "S", 384, 512)
        qz(('p', 0, 0), 0, 128)
        il(('p', 0, 0), "V", 128, 256)
        z_pass(0, 0, 0, 2)
        qz(('p', 0, 0), 256, 384)
        qz(('p', 0, 0), 128, 256)
        square(0, 0, 0)
        qz(('p', 0, 0), 384, 512)
        z_pass(0, 0, 1, 2)
        order_p2(1)
        z_pass(0, 0, 3, 1)
        weigh(0, 0, 0)
        square(0, 0, 1)
        z_pass(0, 0, 2, 2)
        z_pass(0, 0, 3, 2)
        il(('p', 1, 0), "V", 0, 128)
        z_pass(1, 0, 0, 0)
        square(0, 0, 2)
        il(('p', 1, 0), "V", 256, 384)
        z_pass(1, 0, 0, 1)
        qz(('p', 1, 0), 0, 128)
        square(0, 0, 3)
        order_p2(2)
        z_pass(1, 0, 0, 2)
        z_pass(1, 0, 1, 0)
        weigh(0, 0, 1)
        il(('p', 1, 0), "S", 128, 256)
        z_pass(1, 0, 2, 0)
        weigh(0, 0, 3)
        z_pass(1, 0, 1, 1)
        weigh(0, 0, 2)
        square(1, 0, 0)
        il(('p', 2, 0), "V", 0, 128)
        qz(('p', 1, 0), 256, 384)
        il(('p', 1, 0), "S", 384, 512)
        qz(('p', 1, 0), 128, 256)
        il(('h', 0, 0), "V", 0, 256)
        z_pass(1, 0, 1, 2)
        il(('p', 2, 0), "S", 256, 384)
        z_pass(1, 0, 2, 1)
        il(('p', 2, 0), "V", 128, 256)
        z_pass(1, 0, 2, 2)
        il(('h', 0, 0), "V", 256, 512)
        square(1, 0, 1)
        z_pass(1, 0, 3, 0)
        z_pass(2, 0, 0, 0)
        square(1, 0, 2)
        qz(('p', 2, 0), 0, 256)
        z_pass(1, 0, 3, 1)
        qz(('p', 1, 0), 384, 512)
        il(('x', 0, 1), "V", 256, 512)
        il(('x', 0, 1), "S", 0, 256)
        z_pass(1, 0, 3, 2)
        z_pass(2, 0, 0, 1)
        il(('x', 1, 1), "V", 256, 512)
        z_pass(2, 0, 1, 0)
        z_pass(2, 0, 0, 2)
        il(('x', 1, 1), "V", 0, 256)
        z_pass(2, 0, 2, 0)
        il(('p', 2, 0), "S", 384, 512)
        z_pass(2, 0, 1, 1)
        z_pass(2, 0, 1, 2)
        il(('x', 2, 1), "V", 256, 512)
        square(1, 0, 3)
        qz(('x', 1, 1), 0, 512)
        square(2, 0, 0)
        z_pass(2, 0, 3, 0)
        z_pass(2, 0, 2, 1)
        square(2, 0, 1)
        il(('x', 2, 1), "V", 0, 256)
        il(('a', 0, 0), "S", 0, 256)
        qz(('x', 0, 1), 0, 512)
        qz(('p', 2, 0), 256, 512)
        z_pass(0, 1, 0, 0)
        weigh(1, 0, 0)
        z_pass(0, 1, 0, 1)
        il(('a', 1, 0), "S", 256, 512)
        il(('a', 1, 0), "V", 0, 256)
        z_pass(2, 0, 3, 1)
        z_pass(0, 1, 1, 0)
        qz(('x', 2, 1), 0, 512)
        z_pass(0, 1, 1, 1)
        z_pass(2, 0, 2, 2)
        il(('a', 2, 0), "S", 0, 256)
        qz(('h', 0, 0), 0, 512)
        z_pass(0, 1, 1, 2)
        z_pass(2, 0, 3, 2)
        weigh(1, 0, 1)
        weigh(2, 0, 0)
        square(2, 0, 2)
        il(('a', 0, 0), "V", 256, 512)
        square(2, 0, 3)
        weigh(1, 0, 3)
        z_pass(0, 1, 2, 0)
        widen_v()
        qz(('a', 0, 0), 0, 512)
        z_pass(0, 1, 2, 1)
        il(('a', 2, 0), "S", 256, 512)
        z_pass(0, 1, 3, 0)
        weigh(2, 0, 3)
        z_pass(0, 1, 0, 2)
        weigh(1, 0, 2)
        z_pass(0, 1, 3, 1)
        weigh(2, 0, 2)
        l_pass(0, 0, 0)
        square(0, 1, 0)
        weigh(2, 0, 1)
        z_pass(0, 1, 3, 2)
        qz(('a', 1, 0), 0, 512)
        z_pass(0, 1, 2, 2)
        square(0, 1, 1)
        z_pass(1, 1, 0, 0)
        il(('h', 1, 0), "V", 256, 512)
        square(0, 1, 2)
        z_pass(1, 1, 1, 0)
        il(('h', 1, 0), "V", 0, 256)
        z_pass(1, 1, 0, 1)
        square(0, 1, 3)
        z_pass(1, 1, 2, 0)
        z_pass(1, 1, 0, 2)
        weigh(0, 1, 0)
        il(('h', 2, 0), "S", 256, 512)
        z_pass(1, 1, 1, 1)
        weigh(0, 1, 2)
        z_pass(1, 1, 1, 2)
        il(('h', 2, 0), "V", 0, 256)
        l_pass(0, 1, 0)
        z_pass(1, 1, 3, 0)
        weigh(0, 1, 3)
        square(1, 1, 0)
        z_pass(1, 1, 3, 1)
        qz(('h', 1, 0), 0, 512)
        z_pass(1, 1, 3, 2)
        square(1, 1, 1)
        z_pass(1, 1, 2, 1)
        weigh(1, 1, 0)
        z_pass(1, 1, 2, 2)
        weigh(0, 1, 1)
        scale_l0(0, 0, "S")
        z_pass(2, 1, 0, 0)
        qz(('a', 2, 0), 0, 512)
        z_pass(2, 1, 1, 0)
        square(1, 1, 2)
        l_pass(0, 0, 1)
        il(('h', 0, 1), "V", 0, 256)
        l_pass(0, 1, 1)
        square(1, 1, 3)
        z_pass(2, 1, 0, 1)
        qz(('h', 2, 0), 0, 512)
        z_pass(2, 1, 0, 2)
        il(('h', 0, 1), "S", 256, 512)
        z_pass(2, 1, 2, 0)
        weigh(1, 1, 3)
        z_pass(2, 1, 1, 1)
        weigh(1, 1, 2)
        z_pass(2, 1, 3, 0)
        weigh(1, 1, 1)
        z_pass(2, 1, 3, 1)
        scale_l0(0, 1, "V")
        l_pass(0, 1, 2)
        square(2, 1, 0)
        l_pass(0, 2, 0)
        qz(('h', 0, 1), 0, 512)
        z_pass(2, 1, 1, 2)
        il(('h', 1, 1), "S", 256, 512)
        z_pass(2, 1, 2, 1)
        il(('h', 1, 1), "V", 0, 256)
        l_pass(0, 0, 2)
        z_pass(2, 1, 2, 2)
        scale_l0(0, 2, "V")
        z_pass(2, 1, 3, 2)
        weigh(2, 1, 0)
        square(2, 1, 1)
        l_pass(0, 3, 0)
        finish_y(0, 0)
        l_pass(0, 3, 1)
        square(2, 1, 2)
        l_pass(0, 2, 1)
        qz(('h', 1, 1), 0, 512)
        l_pass(1, 0, 0)
        square(2, 1, 3)
        l_pass(0, 2, 2)
        weigh(2, 1, 1)
        l_pass(1, 0, 1)
        weigh(2, 1, 2)
        scale_l0(0, 3, "S")
        l_pass(0, 3, 2)
        weigh(2, 1, 3)
        finish_y(0, 1)
        scale_l0(1, 2, "S")
        il(('h', 2, 1), "V", 256, 384)
        il(('h', 2, 1), "S", 0, 128)
        store_y(0, 1)
        l_pass(1, 1, 0)
        finish_y(0, 2)
        il(('h', 2, 1), "S", 384, 512)
        qz(('h', 2, 1), 256, 384)
        l_pass(1, 2, 0)
        store_y(0, 2)
        il(('h', 2, 1), "V", 128, 256)
        store_y(0, 0)
        scale_l0(1, 3, "S")
        l_pass(1, 2, 1)
        finish_y(0, 3)
        l_pass(1, 2, 2)
        scale_l0(1, 0, "S")
        qz(('h', 2, 1), 0, 128)
        l_pass(1, 3, 0)
        store_y(0, 3)
        qz(('h', 2, 1), 384, 512)
        qz(('h', 2, 1), 128, 256)
        l_pass(1, 0, 2)
        finish_y(1, 2)
        il(('y', 0, 0), "S", 256, 512)
        l_pass(1, 3, 1)
        l_pass(1, 1, 1)
        finish_y(1, 0)
        store_y(1, 2)
        l_pass(1, 3, 2)
        l_pass(1, 1, 2)
        scale_l0(1, 1, "V")
        il(('y', 0, 0), "S", 0, 256)
        store_y(1, 0)
        finish_y(1, 3)
        finish_y(1, 1)
        store_y(1, 3)
        qz(('y', 0, 0), 0, 512)
        il(('y', 1, 0), "S", 128, 256)
        store_y(1, 1)
        il(('y', 1, 0), "V", 0, 128)
        store_codes(0, 0, 512)
        il(('y', 1, 0), "S", 256, 384)
        store_scales(0, range(4))
        il(('y', 1, 0), "V", 384, 512)
        qz(('y', 1, 0), 0, 256)
        qz(('y', 1, 0), 256, 512)
        store_codes(1, 0, 256)
        store_codes(1, 256, 512)
        store_scales(1, range(4))
